import numpy as np
import ml_dtypes


def mxq(x, axis, fmt="e4m3"):
    dtype, down = {"e4m3": (ml_dtypes.float8_e4m3fn, 7), "e5m2": (ml_dtypes.float8_e5m2, 14)}[fmt]
    v = np.moveaxis(np.asarray(x, np.float32).astype(ml_dtypes.bfloat16).astype(np.float64), axis, -1)
    blocks = v.reshape(v.shape[:-1] + (-1, 32))
    amax = np.abs(blocks).max(-1, keepdims=True)
    byte = np.maximum(np.where(amax > 0, np.frexp(amax)[1] - 1 + 127, 0) - down, 1)
    scale = np.exp2(byte - 127.0)
    codes = (blocks / scale).astype(np.float32).astype(dtype).astype(np.float64)
    return np.moveaxis((codes * scale).reshape(v.shape), -1, axis)


WIDE = False


def mx_kscale(k, group=512):
    if not WIDE:
        return np.ones(k)
    levels = np.array([18, -18])
    if group != 512:
        return np.exp2(np.random.permutation(np.resize(levels, k // group))).repeat(group)
    if k % 512:
        return np.exp2(np.random.permutation(np.resize(levels, k // 32))).repeat(32)
    a = np.empty((k // 512, 16))
    for p in range(k // 512):
        a[p, :8] = np.random.permutation(np.resize(levels, 8))
        for g in range(8):
            far = levels[np.abs(levels - a[p, g]) >= 10]
            a[p, g + 8] = far[np.random.randint(len(far))]
    return np.exp2(a.ravel()).repeat(32)


def f64(x):
    return np.asarray(x).astype(np.float64)


def bf(x):
    return np.asarray(x, np.float32).astype(ml_dtypes.bfloat16)


def planes(Y):
    r, m = Y.shape
    b = f64(bf(Y)).reshape(r // 32, 32, m)
    amax = np.abs(b).max(1)
    byte = np.clip(np.where(amax > 0, np.frexp(amax)[1] - 1 + 127 - 7, 1), 1, 254)
    codes = (b * np.exp2(127.0 - byte)[:, None, :]).reshape(r, m).astype(np.float32).astype(ml_dtypes.float8_e4m3fn).view(np.uint8)
    words = codes.reshape(r // 512, 128, 4, m).transpose(0, 1, 3, 2)
    return np.ascontiguousarray(words), np.ascontiguousarray(byte.astype(np.uint8).reshape(r // 512, 16, m))


G, D, M, F, O, N = 4, 128, 128, 128, 128, 512


def sgn(shape):
    return np.random.uniform(0.5, 2.0, shape) * np.where(np.random.standard_normal(shape) < 0, -1.0, 1.0)


def setup_inputs():
    n = np.random.standard_normal
    s_d = mx_kscale(D, 0)
    s_f = mx_kscale(F, 0)
    return {
        "x": (n((G, D, N)) * s_d[:, None]).astype(np.float32),
        "w": (n((G, D, M)) / np.sqrt(D) / s_d[:, None]).astype(np.float32),
        "b": (0.5 * n((G, M, 1))).astype(np.float32),
        "hs": (sgn((G, M, 1)) * np.tile(s_f.reshape(F // G, G).T, (1, G))[:, :, None]).astype(np.float32),
        "v": (n((G, F, O)) / np.sqrt(F) / s_f[:, None]).astype(np.float32),
    }


def reference(x, w, b, hs, v):
    wq = mxq(f64(w), 1, "e4m3")
    xq = mxq(f64(x), 1, "e4m3")
    z = wq.transpose(0, 2, 1) @ xq
    h = np.maximum(z + f64(b), 0.0) * f64(hs)
    u = h.reshape(G * M, N).reshape(G, M, N).transpose(1, 0, 2).reshape(G, M, N)
    vq = mxq(f64(v), 1, "e4m3")
    uq = mxq(u, 1, "e4m3")
    a = vq.transpose(0, 2, 1) @ uq
    Y = a.reshape(G * O, N)
    words, scales = planes(Y)
    return Y, words, scales

@@ -1,0 +1,209 @@
+from contextlib import ExitStack
+
+import concourse.mybir as mybir
+
+F32 = mybir.dt.float32
+BF16 = mybir.dt.bfloat16
+U32 = mybir.dt.uint32
+I32 = mybir.dt.int32
+U8 = mybir.dt.uint8
+FP8X4 = mybir.dt.float8_e4m3fn_x4
+ALU = mybir.AluOpType
+ACT = mybir.ActivationFunctionType
+
+G, D, N = 4, 128, 512
+P = 128
+ROWS = 32
+PACK = 4
+NMM = 128
+FLOPS = 2 * 2 * G * D * D * N
+
+CHUNKS = [(0, 256), (256, 128), (384, 128)]
+
+
+def tile_rows_pl_monarch_relu_bias_kernel(tc, x, w, b, hs, v, out_0, out_1, out_2):
+    nc = tc.nc
+    with ExitStack() as ctx:
+        sb = ctx.enter_context(tc.tile_pool(name="sb", bufs=1))
+        ps = ctx.enter_context(tc.psum_pool(name="ps", bufs=1))
+        ctx.enter_context(tc.manual_schedule())
+
+        def tile(name, shape, dtype):
+            return sb.tile(shape, dtype, name=name, align_bytes=64)
+
+        def packed(name, width):
+            return (
+                tile(name + "_bf", [P, width * PACK], BF16),
+                tile(name + "_codes", [P, width], U32),
+                tile(name + "_scales", [P, width], U8),
+            )
+
+        def words_view(bf, c0, c1):
+            return bf[:, c0 * PACK : c1 * PACK].rearrange("p (c i t) -> p c t i", i=4, t=PACK)
+
+        def rows_view(raw, c0, c1):
+            return raw[:, :, c0:c1].rearrange("p t (c i) -> p c t i", i=4)
+
+        def quantize(bf, codes, scales):
+            nc.vector.quantize_mx(out=codes.bitcast(FP8X4), scales=scales, in_=bf)
+
+        z_bank = [ps.tile([P, N], F32, name="z_bank%d" % g) for g in range(G)]
+        y_bank = [ps.tile([P, N], F32, name="y_bank%d" % g) for g in range(G)]
+
+        w_raw = tile("w_raw", [P, PACK, D], F32)
+        v_raw = tile("v_raw", [P, PACK, D], F32)
+        x_raw = [tile("x_raw%d" % h, [P, PACK, 256], F32) for h in range(2)]
+        rows = tile("rows", [P, P], F32)
+        cols = tile("cols", [P, P], F32)
+        step = tile("step", [P, G], F32)
+        sign = tile("sign", [P, G], F32)
+        mag = tile("mag", [P, G], F32)
+        bmag = tile("bmag", [P, G], F32)
+        w_bf, w_codes, w_scales = packed("w", D)
+        v_bf, v_codes, v_scales = packed("v", D)
+        xq = [packed("x%d" % k, c[1]) for k, c in enumerate(CHUNKS)]
+        uq = [packed("u%d" % k, c[1]) for k, c in enumerate(CHUNKS)]
+        h_bf = [tile("h%d" % k, [P, G, c[1]], BF16) for k, c in enumerate(CHUNKS)]
+        y_f32 = [tile("y%d" % k, [P, G, c[1]], F32) for k, c in enumerate(CHUNKS)]
+        y_dealt = [tile("yd%d" % k, [P, PACK, c[1]], F32) for k, c in enumerate(CHUNKS)]
+        y_bf = [tile("yb%d" % k, [P, c[1] * PACK], BF16) for k, c in enumerate(CHUNKS)]
+        y_codes = tile("y_codes", [P, N], U32)
+        y_scales = tile("y_scales", [P, N], U8)
+
+        x_rows = x.rearrange("g (p j) n -> (g p) j n", j=PACK)
+        for q in range(G):
+            nc.vector.memset(rows[ROWS * q : ROWS * q + 30, :], 0.0)
+        nc.sync.dma_start(out=w_raw[:], in_=w.rearrange("g (p j) m -> (g p) j m", j=PACK))
+        nc.sync.dma_start(out=x_raw[0][:], in_=x_rows[:, :, 0:256])
+        nc.sync.dma_start(out=v_raw[:], in_=v.rearrange("g (p j) o -> (g p) j o", j=PACK))
+        nc.sync.dma_start(out=x_raw[1][:], in_=x_rows[:, :, 256:512])
+        for r, vec in enumerate((b, hs)):
+            nc.scalar.dma_start(
+                out=rows[30 + r : P : ROWS, :].rearrange("q (g i) -> q g i", i=ROWS),
+                in_=vec.rearrange("g (q i) o -> q g (i o)", i=ROWS),
+            )
+        nc.vector.tensor_copy(out=words_view(w_bf, 0, D), in_=rows_view(w_raw, 0, D))
+        nc.vector.transpose(out=cols[:], in_=rows[:])
+        quantize(w_bf[:], w_codes[:], w_scales[:])
+        by_group = cols[:].rearrange("p (g i) -> p g i", i=ROWS)
+        bias = by_group[:, :, 30]
+        gain = by_group[:, :, 31]
+
+        nc.vector.tensor_scalar(out=step[:], in0=gain, scalar1=0.0, scalar2=2.0, op0=ALU.is_ge, op1=ALU.mult)
+        nc.vector.tensor_scalar(out=sign[:], in0=step[:], scalar1=-1.0, scalar2=None, op0=ALU.add)
+        nc.scalar.activation(out=mag[:], in_=gain, func=ACT.Abs)
+        for g in range(G):
+            nc.scalar.activation(out=bmag[:, g : g + 1], in_=bias[:, g : g + 1], func=ACT.Copy, scale=mag[:, g : g + 1])
+
+        def x_interleave(k, a, e, on_scalar):
+            c0 = CHUNKS[k][0]
+            src = rows_view(x_raw[c0 // 256], c0 % 256 + a, c0 % 256 + e)
+            dst = words_view(xq[k][0], a, e)
+            if on_scalar:
+                nc.scalar.copy(out=dst, in_=src)
+            else:
+                nc.vector.tensor_copy(out=dst, in_=src)
+
+        def product(bank, lhs_codes, lhs_scales, rhs, k):
+            c0, width = CHUNKS[k]
+            for j in range(0, width, NMM):
+                for g in range(G):
+                    part = slice(ROWS * g, ROWS * (g + 1))
+                    nc.tensor.matmul_mx(
+                        out=bank[g][:, c0 + j : c0 + j + NMM],
+                        lhsT=lhs_codes[part, :].bitcast(FP8X4),
+                        lhsT_scale=lhs_scales[part, :],
+                        rhs=rhs[1][part, j : j + NMM].bitcast(FP8X4),
+                        rhs_scale=rhs[2][part, j : j + NMM],
+                        start=True,
+                        stop=True,
+                    )
+
+        def x_quant(k):
+            quantize(xq[k][0][:], xq[k][1][:], xq[k][2][:])
+            product(z_bank, w_codes, w_scales, xq[k], k)
+
+        def z_out(k, g, on_scalar):
+            c0, width = CHUNKS[k]
+            src = z_bank[g][:, c0 : c0 + width]
+            if on_scalar:
+                nc.scalar.activation(out=h_bf[k][:, g, :], in_=src, func=ACT.Relu, bias=bmag[:, g : g + 1], scale=mag[:, g : g + 1])
+            else:
+                nc.vector.tensor_scalar(out=h_bf[k][:, g, :], in0=src, scalar1=bias[:, g : g + 1], scalar2=mag[:, g : g + 1], op0=ALU.add, op1=ALU.mult)
+
+        def u_interleave(k):
+            width = CHUNKS[k][1]
+            nc.vector.tensor_scalar(out=words_view(uq[k][0], 0, width), in0=rows_view(h_bf[k], 0, width), scalar1=0.0, scalar2=None, op0=ALU.max)
+
+        def u_quant(k):
+            quantize(uq[k][0][:], uq[k][1][:], uq[k][2][:])
+            product(y_bank, v_codes, v_scales, uq[k], k)
+
+        def y_out(k, g, on_scalar):
+            c0, width = CHUNKS[k]
+            src = y_bank[g][:, c0 : c0 + width]
+            if on_scalar:
+                nc.scalar.copy(out=y_f32[k][:, g, :], in_=src)
+            else:
+                nc.vector.tensor_copy(out=y_f32[k][:, g, :], in_=src)
+            nc.sync.dma_start(out=y_dealt[k][ROWS * g : ROWS * (g + 1), :, :], in_=y_f32[k][:, g, :])
+
+        def y_store(k):
+            c0, width = CHUNKS[k]
+            nc.sync.dma_start(out=out_0.rearrange("(g o) n -> o g n", g=G)[:, :, c0 : c0 + width], in_=y_f32[k][:])
+
+        def y_interleave(k):
+            width = CHUNKS[k][1]
+            nc.vector.tensor_copy(out=words_view(y_bf[k], 0, width), in_=rows_view(y_dealt[k], 0, width))
+
+        def y_quant(k):
+            c0, width = CHUNKS[k]
+            quantize(y_bf[k][:], y_codes[:, c0 : c0 + width], y_scales[:, c0 : c0 + width])
+            words = out_1.rearrange("r p n s -> (r p) (n s)").bitcast(I32)
+            nc.sync.dma_start(out=words[:, c0 : c0 + width], in_=y_codes[:, c0 : c0 + width].bitcast(I32))
+
+        x_interleave(0, 0, 176, False)
+        x_interleave(0, 176, 256, True)
+        x_quant(0)
+        nc.vector.tensor_tensor(
+            out=v_bf[:].rearrange("p (o t) -> p o t", t=PACK),
+            in0=v_raw[:].rearrange("p t o -> p o t"),
+            in1=sign[:].unsqueeze(1).to_broadcast([P, D, PACK]),
+            op=ALU.mult,
+        )
+        x_interleave(1, 0, 128, False)
+        quantize(v_bf[:], v_codes[:], v_scales[:])
+        x_quant(1)
+        for g in range(G):
+            z_out(0, g, True)
+        x_interleave(2, 0, 128, False)
+        u_interleave(0)
+        x_quant(2)
+        u_quant(0)
+        for g in range(G):
+            z_out(1, g, True)
+        u_interleave(1)
+        for g in range(G):
+            z_out(2, g, True)
+        u_quant(1)
+        u_interleave(2)
+        for g in range(G):
+            y_out(0, g, g != 0)
+        u_quant(2)
+        y_store(0)
+        for g in range(G):
+            y_out(1, g, g >= 2)
+        for g in range(G):
+            y_out(2, g, g >= 2)
+        y_store(1)
+        y_store(2)
+        y_interleave(0)
+        y_interleave(1)
+        y_quant(0)
+        y_quant(1)
+        y_interleave(2)
+        y_quant(2)
+        scale_rows = out_2.rearrange("r t n -> (r t) n").bitcast(I32)
+        for q in range(G):
+            queue = nc.scalar if q % 2 else nc.sync
+            queue.dma_start(out=scale_rows[4 * q : 4 * q + 4, :], in_=y_scales[ROWS * q : ROWS * q + 4, :].bitcast(I32))

@@ -18,7 +18,10 @@ PACK = 4
 NMM = 128
 FLOPS = 2 * 2 * G * D * D * N
 
+HALF = N // 2
 CHUNKS = [(0, 256), (256, 128), (384, 128)]
+Z_BANK = (0, 1, 1)
+Y_BANK = (0, 1, 0)
 
 
 def tile_rows_pl_monarch_relu_bias_kernel(tc, x, w, b, hs, v, out_0, out_1, out_2):
@@ -44,27 +47,26 @@ def tile_rows_pl_monarch_relu_bias_kernel(tc, x, w, b, hs, v, out_0, out_1, out_
         def rows_view(raw, c0, c1):
             return raw[:, :, c0:c1].rearrange("p t (c i) -> p c t i", i=4)
 
-        def quantize(bf, codes, scales):
-            nc.vector.quantize_mx(out=codes.bitcast(FP8X4), scales=scales, in_=bf)
+        def quantize(trio):
+            nc.vector.quantize_mx(out=trio[1][:].bitcast(FP8X4), scales=trio[2][:], in_=trio[0][:])
 
-        z_bank = [ps.tile([P, N], F32, name="z_bank%d" % g) for g in range(G)]
-        y_bank = [ps.tile([P, N], F32, name="y_bank%d" % g) for g in range(G)]
+        banks = [[ps.tile([P, N], F32, name="bank_%s%d" % (s, g)) for g in range(G)] for s in "ab"]
 
         w_raw = tile("w_raw", [P, PACK, D], F32)
         v_raw = tile("v_raw", [P, PACK, D], F32)
-        x_raw = [tile("x_raw%d" % h, [P, PACK, 256], F32) for h in range(2)]
+        x_raw = [tile("x_raw%d" % h, [P, PACK, HALF], F32) for h in range(2)]
         rows = tile("rows", [P, P], F32)
         cols = tile("cols", [P, P], F32)
         step = tile("step", [P, G], F32)
         sign = tile("sign", [P, G], F32)
         mag = tile("mag", [P, G], F32)
         bmag = tile("bmag", [P, G], F32)
-        w_bf, w_codes, w_scales = packed("w", D)
-        v_bf, v_codes, v_scales = packed("v", D)
+        wq = packed("w", D)
+        vq = packed("v", D)
         xq = [packed("x%d" % k, c[1]) for k, c in enumerate(CHUNKS)]
         uq = [packed("u%d" % k, c[1]) for k, c in enumerate(CHUNKS)]
         h_bf = [tile("h%d" % k, [P, G, c[1]], BF16) for k, c in enumerate(CHUNKS)]
-        y_f32 = [tile("y%d" % k, [P, G, c[1]], F32) for k, c in enumerate(CHUNKS)]
+        y_f32 = tile("y", [P, G, N], F32)
         y_dealt = [tile("yd%d" % k, [P, PACK, c[1]], F32) for k, c in enumerate(CHUNKS)]
         y_bf = [tile("yb%d" % k, [P, c[1] * PACK], BF16) for k, c in enumerate(CHUNKS)]
         y_codes = tile("y_codes", [P, N], U32)
@@ -73,137 +75,147 @@ def tile_rows_pl_monarch_relu_bias_kernel(tc, x, w, b, hs, v, out_0, out_1, out_
         x_rows = x.rearrange("g (p j) n -> (g p) j n", j=PACK)
         for q in range(G):
             nc.vector.memset(rows[ROWS * q : ROWS * q + 30, :], 0.0)
-        nc.sync.dma_start(out=w_raw[:], in_=w.rearrange("g (p j) m -> (g p) j m", j=PACK))
-        nc.sync.dma_start(out=x_raw[0][:], in_=x_rows[:, :, 0:256])
-        nc.sync.dma_start(out=v_raw[:], in_=v.rearrange("g (p j) o -> (g p) j o", j=PACK))
-        nc.sync.dma_start(out=x_raw[1][:], in_=x_rows[:, :, 256:512])
         for r, vec in enumerate((b, hs)):
-            nc.scalar.dma_start(
+            nc.sync.dma_start(
                 out=rows[30 + r : P : ROWS, :].rearrange("q (g i) -> q g i", i=ROWS),
                 in_=vec.rearrange("g (q i) o -> q g (i o)", i=ROWS),
             )
-        nc.vector.tensor_copy(out=words_view(w_bf, 0, D), in_=rows_view(w_raw, 0, D))
+        nc.sync.dma_start(out=w_raw[:], in_=w.rearrange("g (p j) m -> (g p) j m", j=PACK))
+        nc.sync.dma_start(out=x_raw[0][:], in_=x_rows[:, :, 0:HALF])
+        nc.sync.dma_start(out=x_raw[1][:], in_=x_rows[:, :, HALF:N])
+        nc.sync.dma_start(out=v_raw[:], in_=v.rearrange("g (p j) o -> (g p) j o", j=PACK))
         nc.vector.transpose(out=cols[:], in_=rows[:])
-        quantize(w_bf[:], w_codes[:], w_scales[:])
         by_group = cols[:].rearrange("p (g i) -> p g i", i=ROWS)
         bias = by_group[:, :, 30]
         gain = by_group[:, :, 31]
-
         nc.vector.tensor_scalar(out=step[:], in0=gain, scalar1=0.0, scalar2=2.0, op0=ALU.is_ge, op1=ALU.mult)
+        nc.vector.tensor_copy(out=words_view(wq[0], 0, D), in_=rows_view(w_raw, 0, D))
         nc.vector.tensor_scalar(out=sign[:], in0=step[:], scalar1=-1.0, scalar2=None, op0=ALU.add)
+        quantize(wq)
         nc.scalar.activation(out=mag[:], in_=gain, func=ACT.Abs)
         for g in range(G):
             nc.scalar.activation(out=bmag[:, g : g + 1], in_=bias[:, g : g + 1], func=ACT.Copy, scale=mag[:, g : g + 1])
 
         def x_interleave(k, a, e, on_scalar):
             c0 = CHUNKS[k][0]
-            src = rows_view(x_raw[c0 // 256], c0 % 256 + a, c0 % 256 + e)
-            dst = words_view(xq[k][0], a, e)
-            if on_scalar:
-                nc.scalar.copy(out=dst, in_=src)
-            else:
-                nc.vector.tensor_copy(out=dst, in_=src)
+            copy = nc.scalar.copy if on_scalar else nc.vector.tensor_copy
+            copy(out=words_view(xq[k][0], a, e), in_=rows_view(x_raw[c0 // HALF], c0 % HALF + a, c0 % HALF + e))
 
-        def product(bank, lhs_codes, lhs_scales, rhs, k):
+        def v_interleave():
+            nc.vector.tensor_tensor(
+                out=vq[0][:].rearrange("p (o t) -> p o t", t=PACK),
+                in0=v_raw[:].rearrange("p t o -> p o t"),
+                in1=sign[:].unsqueeze(1).to_broadcast([P, D, PACK]),
+                op=ALU.mult,
+            )
+
+        def product(bank, weights, acts, k):
             c0, width = CHUNKS[k]
             for j in range(0, width, NMM):
                 for g in range(G):
                     part = slice(ROWS * g, ROWS * (g + 1))
                     nc.tensor.matmul_mx(
                         out=bank[g][:, c0 + j : c0 + j + NMM],
-                        lhsT=lhs_codes[part, :].bitcast(FP8X4),
-                        lhsT_scale=lhs_scales[part, :],
-                        rhs=rhs[1][part, j : j + NMM].bitcast(FP8X4),
-                        rhs_scale=rhs[2][part, j : j + NMM],
+                        lhsT=weights[1][part, :].bitcast(FP8X4),
+                        lhsT_scale=weights[2][part, :],
+                        rhs=acts[1][part, j : j + NMM].bitcast(FP8X4),
+                        rhs_scale=acts[2][part, j : j + NMM],
                         start=True,
                         stop=True,
                     )
 
         def x_quant(k):
-            quantize(xq[k][0][:], xq[k][1][:], xq[k][2][:])
-            product(z_bank, w_codes, w_scales, xq[k], k)
+            quantize(xq[k])
+            product(banks[Z_BANK[k]], wq, xq[k], k)
 
         def z_out(k, g, on_scalar):
             c0, width = CHUNKS[k]
-            src = z_bank[g][:, c0 : c0 + width]
+            src = banks[Z_BANK[k]][g][:, c0 : c0 + width]
             if on_scalar:
                 nc.scalar.activation(out=h_bf[k][:, g, :], in_=src, func=ACT.Relu, bias=bmag[:, g : g + 1], scale=mag[:, g : g + 1])
             else:
                 nc.vector.tensor_scalar(out=h_bf[k][:, g, :], in0=src, scalar1=bias[:, g : g + 1], scalar2=mag[:, g : g + 1], op0=ALU.add, op1=ALU.mult)
 
-        def u_interleave(k):
-            width = CHUNKS[k][1]
-            nc.vector.tensor_scalar(out=words_view(uq[k][0], 0, width), in0=rows_view(h_bf[k], 0, width), scalar1=0.0, scalar2=None, op0=ALU.max)
+        def u_interleave(k, a, e, on_scalar):
+            dst = words_view(uq[k][0], a, e)
+            src = rows_view(h_bf[k], a, e)
+            if on_scalar:
+                nc.scalar.activation(out=dst, in_=src, func=ACT.Relu)
+            else:
+                nc.vector.tensor_scalar(out=dst, in0=src, scalar1=0.0, scalar2=None, op0=ALU.max)
 
         def u_quant(k):
-            quantize(uq[k][0][:], uq[k][1][:], uq[k][2][:])
-            product(y_bank, v_codes, v_scales, uq[k], k)
+            quantize(uq[k])
+            product(banks[Y_BANK[k]], vq, uq[k], k)
 
         def y_out(k, g, on_scalar):
             c0, width = CHUNKS[k]
-            src = y_bank[g][:, c0 : c0 + width]
-            if on_scalar:
-                nc.scalar.copy(out=y_f32[k][:, g, :], in_=src)
-            else:
-                nc.vector.tensor_copy(out=y_f32[k][:, g, :], in_=src)
-            nc.sync.dma_start(out=y_dealt[k][ROWS * g : ROWS * (g + 1), :, :], in_=y_f32[k][:, g, :])
+            copy = nc.scalar.copy if on_scalar else nc.vector.tensor_copy
+            copy(out=y_f32[:, g, c0 : c0 + width], in_=banks[Y_BANK[k]][g][:, c0 : c0 + width])
+            nc.sync.dma_start(out=y_dealt[k][ROWS * g : ROWS * (g + 1), :, :], in_=y_f32[:, g, c0 : c0 + width])
 
-        def y_store(k):
-            c0, width = CHUNKS[k]
-            nc.sync.dma_start(out=out_0.rearrange("(g o) n -> o g n", g=G)[:, :, c0 : c0 + width], in_=y_f32[k][:])
+        def y_store(c0, c1):
+            nc.sync.dma_start(out=out_0.rearrange("(g o) n -> o g n", g=G)[:, :, c0:c1], in_=y_f32[:, :, c0:c1])
 
-        def y_interleave(k):
-            width = CHUNKS[k][1]
-            nc.vector.tensor_copy(out=words_view(y_bf[k], 0, width), in_=rows_view(y_dealt[k], 0, width))
+        def y_interleave(k, a, e, on_scalar):
+            copy = nc.scalar.copy if on_scalar else nc.vector.tensor_copy
+            copy(out=words_view(y_bf[k], a, e), in_=rows_view(y_dealt[k], a, e))
 
         def y_quant(k):
             c0, width = CHUNKS[k]
-            quantize(y_bf[k][:], y_codes[:, c0 : c0 + width], y_scales[:, c0 : c0 + width])
+            nc.vector.quantize_mx(
+                out=y_codes[:, c0 : c0 + width].bitcast(FP8X4), scales=y_scales[:, c0 : c0 + width], in_=y_bf[k][:]
+            )
+
+        def words_store(c0, c1):
             words = out_1.rearrange("r p n s -> (r p) (n s)").bitcast(I32)
-            nc.sync.dma_start(out=words[:, c0 : c0 + width], in_=y_codes[:, c0 : c0 + width].bitcast(I32))
+            nc.sync.dma_start(out=words[:, c0:c1], in_=y_codes[:, c0:c1].bitcast(I32))
+
+        def scales_store(q, queue):
+            scale_rows = out_2.rearrange("r t n -> (r t) n").bitcast(I32)
+            queue.dma_start(out=scale_rows[4 * q : 4 * q + 4, :], in_=y_scales[ROWS * q : ROWS * q + 4, :].bitcast(I32))
 
         x_interleave(0, 0, 176, False)
         x_interleave(0, 176, 256, True)
         x_quant(0)
-        nc.vector.tensor_tensor(
-            out=v_bf[:].rearrange("p (o t) -> p o t", t=PACK),
-            in0=v_raw[:].rearrange("p t o -> p o t"),
-            in1=sign[:].unsqueeze(1).to_broadcast([P, D, PACK]),
-            op=ALU.mult,
-        )
         x_interleave(1, 0, 128, False)
-        quantize(v_bf[:], v_codes[:], v_scales[:])
+        x_interleave(2, 0, 128, True)
         x_quant(1)
-        for g in range(G):
-            z_out(0, g, True)
-        x_interleave(2, 0, 128, False)
-        u_interleave(0)
         x_quant(2)
-        u_quant(0)
+        z_out(0, 0, True)
+        v_interleave()
+        z_out(0, 1, True)
+        z_out(0, 2, True)
+        z_out(0, 3, False)
+        quantize(vq)
+        u_interleave(0, 0, 256, False)
         for g in range(G):
             z_out(1, g, True)
-        u_interleave(1)
+        u_quant(0)
+        u_interleave(1, 0, 128, False)
         for g in range(G):
             z_out(2, g, True)
         u_quant(1)
-        u_interleave(2)
+        u_interleave(2, 0, 128, False)
+        for g in range(3):
+            y_out(0, g, True)
+        quantize(uq[2])
+        y_out(0, 3, False)
+        product(banks[Y_BANK[2]], vq, uq[2], 2)
         for g in range(G):
-            y_out(0, g, g != 0)
-        u_quant(2)
-        y_store(0)
+            y_out(1, g, g % 2 == 0)
         for g in range(G):
-            y_out(1, g, g >= 2)
-        for g in range(G):
-            y_out(2, g, g >= 2)
-        y_store(1)
-        y_store(2)
-        y_interleave(0)
-        y_interleave(1)
+            y_out(2, g, g % 2 == 0)
+        y_store(0, N)
+        y_interleave(0, 0, 176, False)
+        y_interleave(0, 176, 256, True)
         y_quant(0)
+        words_store(0, 256)
+        y_interleave(1, 0, 128, False)
+        y_interleave(2, 0, 48, True)
+        y_interleave(2, 48, 128, False)
         y_quant(1)
-        y_interleave(2)
         y_quant(2)
-        scale_rows = out_2.rearrange("r t n -> (r t) n").bitcast(I32)
+        words_store(256, N)
         for q in range(G):
-            queue = nc.scalar if q % 2 else nc.sync
-            queue.dma_start(out=scale_rows[4 * q : 4 * q + 4, :], in_=y_scales[ROWS * q : ROWS * q + 4, :].bitcast(I32))
+            scales_store(q, nc.sync if q == 0 else nc.scalar)

@@ -15,13 +15,12 @@ G, D, N = 4, 128, 512
 P = 128
 ROWS = 32
 PACK = 4
-NMM = 128
 FLOPS = 2 * 2 * G * D * D * N
 
 HALF = N // 2
-CHUNKS = [(0, 256), (256, 128), (384, 128)]
-Z_BANK = (0, 1, 1)
-Y_BANK = (0, 1, 0)
+CHUNKS = [(0, 256), (256, 256)]
+Z_BANK = (0, 1)
+Y_BANK = (0, 1)
 
 
 def tile_rows_pl_monarch_relu_bias_kernel(tc, x, w, b, hs, v, out_0, out_1, out_2):
@@ -63,35 +62,44 @@ def tile_rows_pl_monarch_relu_bias_kernel(tc, x, w, b, hs, v, out_0, out_1, out_
         bmag = tile("bmag", [P, G], F32)
         wq = packed("w", D)
         vq = packed("v", D)
-        xq = [packed("x%d" % k, c[1]) for k, c in enumerate(CHUNKS)]
-        uq = [packed("u%d" % k, c[1]) for k, c in enumerate(CHUNKS)]
+        act_codes = tile("act_codes", [P, 5 * HALF], U32)
+        act_scales = tile("act_scales", [P, 5 * HALF], U8)
+
+        def window(name, slot):
+            cols = slice(slot * HALF, (slot + 1) * HALF)
+            return (tile(name, [P, HALF * PACK], BF16), act_codes[:, cols], act_scales[:, cols])
+
+        xq = [window("x_bf%d" % k, 1 + k) for k in range(2)]
+        uq = [window("u_bf%d" % k, 3 + k) for k in range(2)]
         h_bf = [tile("h%d" % k, [P, G, c[1]], BF16) for k, c in enumerate(CHUNKS)]
         y_f32 = tile("y", [P, G, N], F32)
-        y_dealt = [tile("yd%d" % k, [P, PACK, c[1]], F32) for k, c in enumerate(CHUNKS)]
+        y_round = [tile("yr%d" % k, [P, G, c[1]], BF16) for k, c in enumerate(CHUNKS)]
+        y_dealt = [tile("yd%d" % k, [P, PACK, c[1]], BF16) for k, c in enumerate(CHUNKS)]
         y_bf = [tile("yb%d" % k, [P, c[1] * PACK], BF16) for k, c in enumerate(CHUNKS)]
         y_codes = tile("y_codes", [P, N], U32)
         y_scales = tile("y_scales", [P, N], U8)
 
         x_rows = x.rearrange("g (p j) n -> (g p) j n", j=PACK)
-        for q in range(G):
-            nc.vector.memset(rows[ROWS * q : ROWS * q + 30, :], 0.0)
+        nc.vector.memset(rows[:], 0.0)
+        nc.sync.dma_start(out=w_raw[:], in_=w.rearrange("g (p j) m -> (g p) j m", j=PACK))
         for r, vec in enumerate((b, hs)):
             nc.sync.dma_start(
-                out=rows[30 + r : P : ROWS, :].rearrange("q (g i) -> q g i", i=ROWS),
+                out=rows[r:P:ROWS, :].rearrange("q (g i) -> q g i", i=ROWS),
                 in_=vec.rearrange("g (q i) o -> q g (i o)", i=ROWS),
             )
-        nc.sync.dma_start(out=w_raw[:], in_=w.rearrange("g (p j) m -> (g p) j m", j=PACK))
         nc.sync.dma_start(out=x_raw[0][:], in_=x_rows[:, :, 0:HALF])
         nc.sync.dma_start(out=x_raw[1][:], in_=x_rows[:, :, HALF:N])
         nc.sync.dma_start(out=v_raw[:], in_=v.rearrange("g (p j) o -> (g p) j o", j=PACK))
-        nc.vector.transpose(out=cols[:], in_=rows[:])
-        by_group = cols[:].rearrange("p (g i) -> p g i", i=ROWS)
-        bias = by_group[:, :, 30]
-        gain = by_group[:, :, 31]
-        nc.vector.tensor_scalar(out=step[:], in0=gain, scalar1=0.0, scalar2=2.0, op0=ALU.is_ge, op1=ALU.mult)
+        nc.vector.memset(act_codes[:, 0:HALF], 0)
+        nc.vector.memset(act_scales[:, 0:HALF], 0)
         nc.vector.tensor_copy(out=words_view(wq[0], 0, D), in_=rows_view(w_raw, 0, D))
-        nc.vector.tensor_scalar(out=sign[:], in0=step[:], scalar1=-1.0, scalar2=None, op0=ALU.add)
+        nc.vector.transpose(out=cols[:], in_=rows[:])
         quantize(wq)
+        by_group = cols[:].rearrange("p (g i) -> p g i", i=ROWS)
+        bias = by_group[:, :, 0]
+        gain = by_group[:, :, 1]
+        nc.vector.tensor_scalar(out=step[:], in0=gain, scalar1=0.0, scalar2=2.0, op0=ALU.is_ge, op1=ALU.mult)
+        nc.vector.tensor_scalar(out=sign[:], in0=step[:], scalar1=-1.0, scalar2=None, op0=ALU.add)
         nc.scalar.activation(out=mag[:], in_=gain, func=ACT.Abs)
         for g in range(G):
             nc.scalar.activation(out=bmag[:, g : g + 1], in_=bias[:, g : g + 1], func=ACT.Copy, scale=mag[:, g : g + 1])
@@ -103,34 +111,33 @@ def tile_rows_pl_monarch_relu_bias_kernel(tc, x, w, b, hs, v, out_0, out_1, out_
 
         def v_interleave():
             nc.vector.tensor_tensor(
-                out=vq[0][:].rearrange("p (o t) -> p o t", t=PACK),
-                in0=v_raw[:].rearrange("p t o -> p o t"),
-                in1=sign[:].unsqueeze(1).to_broadcast([P, D, PACK]),
+                out=words_view(vq[0], 0, D),
+                in0=rows_view(v_raw, 0, D),
+                in1=sign[:].unsqueeze(1).unsqueeze(3).to_broadcast([P, D // 4, PACK, 4]),
                 op=ALU.mult,
             )
 
-        def product(bank, weights, acts, k):
-            c0, width = CHUNKS[k]
-            for j in range(0, width, NMM):
-                for g in range(G):
-                    part = slice(ROWS * g, ROWS * (g + 1))
-                    nc.tensor.matmul_mx(
-                        out=bank[g][:, c0 + j : c0 + j + NMM],
-                        lhsT=weights[1][part, :].bitcast(FP8X4),
-                        lhsT_scale=weights[2][part, :],
-                        rhs=acts[1][part, j : j + NMM].bitcast(FP8X4),
-                        rhs_scale=acts[2][part, j : j + NMM],
-                        start=True,
-                        stop=True,
-                    )
+        def product(bank, weights, slot):
+            cols = slice((slot - 1) * HALF, (slot + 1) * HALF)
+            for g in range(G):
+                part = slice(ROWS * g, ROWS * (g + 1))
+                nc.tensor.matmul_mx(
+                    out=bank[g][:],
+                    lhsT=weights[1][part, :].bitcast(FP8X4),
+                    lhsT_scale=weights[2][part, :],
+                    rhs=act_codes[part, cols].bitcast(FP8X4),
+                    rhs_scale=act_scales[part, cols],
+                    start=True,
+                    stop=True,
+                )
 
         def x_quant(k):
             quantize(xq[k])
-            product(banks[Z_BANK[k]], wq, xq[k], k)
+            product(banks[Z_BANK[k]], wq, 1 + k)
 
         def z_out(k, g, on_scalar):
             c0, width = CHUNKS[k]
-            src = banks[Z_BANK[k]][g][:, c0 : c0 + width]
+            src = banks[Z_BANK[k]][g][:, HALF:N]
             if on_scalar:
                 nc.scalar.activation(out=h_bf[k][:, g, :], in_=src, func=ACT.Relu, bias=bmag[:, g : g + 1], scale=mag[:, g : g + 1])
             else:
@@ -146,16 +153,21 @@ def tile_rows_pl_monarch_relu_bias_kernel(tc, x, w, b, hs, v, out_0, out_1, out_
 
         def u_quant(k):
             quantize(uq[k])
-            product(banks[Y_BANK[k]], vq, uq[k], k)
+            product(banks[Y_BANK[k]], vq, 3 + k)
 
         def y_out(k, g, on_scalar):
             c0, width = CHUNKS[k]
             copy = nc.scalar.copy if on_scalar else nc.vector.tensor_copy
-            copy(out=y_f32[:, g, c0 : c0 + width], in_=banks[Y_BANK[k]][g][:, c0 : c0 + width])
-            nc.sync.dma_start(out=y_dealt[k][ROWS * g : ROWS * (g + 1), :, :], in_=y_f32[:, g, c0 : c0 + width])
+            copy(out=y_f32[:, g, c0 : c0 + width], in_=banks[Y_BANK[k]][g][:, HALF:N])
 
-        def y_store(c0, c1):
-            nc.sync.dma_start(out=out_0.rearrange("(g o) n -> o g n", g=G)[:, :, c0:c1], in_=y_f32[:, :, c0:c1])
+        def y_deal(k, g, on_scalar):
+            c0, width = CHUNKS[k]
+            copy = nc.scalar.copy if on_scalar else nc.vector.tensor_copy
+            copy(out=y_round[k][:, g, :], in_=banks[Y_BANK[k]][g][:, HALF:N])
+            nc.sync.dma_start(out=y_dealt[k][ROWS * g : ROWS * (g + 1), :, :], in_=y_round[k][:, g, :])
+
+        def y_store(g0, g1):
+            nc.sync.dma_start(out=out_0.rearrange("(g o) n -> o g n", g=G)[:, g0:g1, :], in_=y_f32[:, g0:g1, :])
 
         def y_interleave(k, a, e, on_scalar):
             copy = nc.scalar.copy if on_scalar else nc.vector.tensor_copy
@@ -169,53 +181,49 @@ def tile_rows_pl_monarch_relu_bias_kernel(tc, x, w, b, hs, v, out_0, out_1, out_
 
         def words_store(c0, c1):
             words = out_1.rearrange("r p n s -> (r p) (n s)").bitcast(I32)
-            nc.sync.dma_start(out=words[:, c0:c1], in_=y_codes[:, c0:c1].bitcast(I32))
+            nc.scalar.dma_start(out=words[:, c0:c1], in_=y_codes[:, c0:c1].bitcast(I32))
 
         def scales_store(q, queue):
             scale_rows = out_2.rearrange("r t n -> (r t) n").bitcast(I32)
             queue.dma_start(out=scale_rows[4 * q : 4 * q + 4, :], in_=y_scales[ROWS * q : ROWS * q + 4, :].bitcast(I32))
 
         x_interleave(0, 0, 176, False)
-        x_interleave(0, 176, 256, True)
+        x_interleave(0, 176, HALF, True)
         x_quant(0)
-        x_interleave(1, 0, 128, False)
-        x_interleave(2, 0, 128, True)
+        x_interleave(1, 0, 176, False)
+        x_interleave(1, 176, HALF, True)
         x_quant(1)
-        x_quant(2)
-        z_out(0, 0, True)
         v_interleave()
-        z_out(0, 1, True)
-        z_out(0, 2, True)
-        z_out(0, 3, False)
+        for g in range(G):
+            z_out(0, g, g < 3)
         quantize(vq)
-        u_interleave(0, 0, 256, False)
+        u_interleave(0, 0, HALF, False)
         for g in range(G):
-            z_out(1, g, True)
+            z_out(1, g, g < 3)
         u_quant(0)
-        u_interleave(1, 0, 128, False)
-        for g in range(G):
-            z_out(2, g, True)
+        u_interleave(1, 0, 176, False)
+        u_interleave(1, 176, HALF, True)
         u_quant(1)
-        u_interleave(2, 0, 128, False)
-        for g in range(3):
-            y_out(0, g, True)
-        quantize(uq[2])
-        y_out(0, 3, False)
-        product(banks[Y_BANK[2]], vq, uq[2], 2)
         for g in range(G):
+            y_deal(0, g, g % 2 == 0)
+        for g in range(2):
+            y_out(0, g, g % 2 == 0)
+        for g in range(G):
+            y_deal(1, g, g % 2 == 0)
+        for g in range(2):
             y_out(1, g, g % 2 == 0)
-        for g in range(G):
-            y_out(2, g, g % 2 == 0)
-        y_store(0, N)
+        y_store(0, 2)
+        for k in range(2):
+            for g in range(2, 4):
+                y_out(k, g, g % 2 == 0)
+        y_store(2, 4)
         y_interleave(0, 0, 176, False)
-        y_interleave(0, 176, 256, True)
+        y_interleave(0, 176, HALF, True)
         y_quant(0)
-        words_store(0, 256)
-        y_interleave(1, 0, 128, False)
-        y_interleave(2, 0, 48, True)
-        y_interleave(2, 48, 128, False)
+        y_interleave(1, 0, 176, False)
+        y_interleave(1, 176, HALF, True)
+        words_store(0, HALF)
         y_quant(1)
-        y_quant(2)
-        words_store(256, N)
+        words_store(HALF, N)
         for q in range(G):
-            scales_store(q, nc.sync if q == 0 else nc.scalar)
+            scales_store(q, nc.sync if q < 2 else nc.scalar)

@@ -190,12 +190,15 @@ def tile_rows_pl_monarch_relu_bias_kernel(tc, x, w, b, hs, v, out_0, out_1, out_
         x_interleave(0, 0, 176, False)
         x_interleave(0, 176, HALF, True)
         x_quant(0)
+        product(banks[1], wq, 1)
         x_interleave(1, 0, 176, False)
         x_interleave(1, 176, HALF, True)
         x_quant(1)
         v_interleave()
         for g in range(G):
             z_out(0, g, g < 3)
+        product(banks[0], wq, 2)
+        product(banks[0], wq, 2)
         quantize(vq)
         u_interleave(0, 0, HALF, False)
         for g in range(G):

from contextlib import ExitStack

import concourse.mybir as mybir

F32 = mybir.dt.float32
BF16 = mybir.dt.bfloat16
U32 = mybir.dt.uint32
I32 = mybir.dt.int32
U8 = mybir.dt.uint8
FP8X4 = mybir.dt.float8_e4m3fn_x4
ALU = mybir.AluOpType
ACT = mybir.ActivationFunctionType

G, D, N = 4, 128, 512
P = 128
ROWS = 32
PACK = 4
FLOPS = 2 * 2 * G * D * D * N

HALF = N // 2
CHUNKS = [(0, 256), (256, 256)]
Z_BANK = (0, 1)
Y_BANK = (0, 1)


def tile_rows_pl_monarch_relu_bias_kernel(tc, x, w, b, hs, v, out_0, out_1, out_2):
    nc = tc.nc
    with ExitStack() as ctx:
        sb = ctx.enter_context(tc.tile_pool(name="sb", bufs=1))
        ps = ctx.enter_context(tc.psum_pool(name="ps", bufs=1))
        ctx.enter_context(tc.manual_schedule())

        def tile(name, shape, dtype):
            return sb.tile(shape, dtype, name=name, align_bytes=64)

        def packed(name, width):
            return (
                tile(name + "_bf", [P, width * PACK], BF16),
                tile(name + "_codes", [P, width], U32),
                tile(name + "_scales", [P, width], U8),
            )

        def words_view(bf, c0, c1):
            return bf[:, c0 * PACK : c1 * PACK].rearrange("p (c i t) -> p c t i", i=4, t=PACK)

        def rows_view(raw, c0, c1):
            return raw[:, :, c0:c1].rearrange("p t (c i) -> p c t i", i=4)

        def quantize(trio):
            nc.vector.quantize_mx(out=trio[1][:].bitcast(FP8X4), scales=trio[2][:], in_=trio[0][:])

        banks = [[ps.tile([P, N], F32, name="bank_%s%d" % (s, g)) for g in range(G)] for s in "ab"]

        w_raw = tile("w_raw", [P, PACK, D], F32)
        v_raw = tile("v_raw", [P, PACK, D], F32)
        x_raw = [tile("x_raw%d" % h, [P, PACK, HALF], F32) for h in range(2)]
        rows = tile("rows", [P, P], F32)
        cols = tile("cols", [P, P], F32)
        step = tile("step", [P, G], F32)
        sign = tile("sign", [P, G], F32)
        mag = tile("mag", [P, G], F32)
        bmag = tile("bmag", [P, G], F32)
        wq = packed("w", D)
        vq = packed("v", D)
        act_codes = tile("act_codes", [P, 5 * HALF], U32)
        act_scales = tile("act_scales", [P, 5 * HALF], U8)

        def window(name, slot):
            cols = slice(slot * HALF, (slot + 1) * HALF)
            return (tile(name, [P, HALF * PACK], BF16), act_codes[:, cols], act_scales[:, cols])

        xq = [window("x_bf%d" % k, 1 + k) for k in range(2)]
        uq = [window("u_bf%d" % k, 3 + k) for k in range(2)]
        h_bf = [tile("h%d" % k, [P, G, c[1]], BF16) for k, c in enumerate(CHUNKS)]
        y_f32 = tile("y", [P, G, N], F32)
        y_round = [tile("yr%d" % k, [P, G, c[1]], BF16) for k, c in enumerate(CHUNKS)]
        y_dealt = [tile("yd%d" % k, [P, PACK, c[1]], BF16) for k, c in enumerate(CHUNKS)]
        y_bf = [tile("yb%d" % k, [P, c[1] * PACK], BF16) for k, c in enumerate(CHUNKS)]
        y_codes = tile("y_codes", [P, N], U32)
        y_scales = tile("y_scales", [P, N], U8)

        x_rows = x.rearrange("g (p j) n -> (g p) j n", j=PACK)
        nc.vector.memset(rows[:], 0.0)
        nc.sync.dma_start(out=w_raw[:], in_=w.rearrange("g (p j) m -> (g p) j m", j=PACK))
        for r, vec in enumerate((b, hs)):
            nc.sync.dma_start(
                out=rows[r:P:ROWS, :].rearrange("q (g i) -> q g i", i=ROWS),
                in_=vec.rearrange("g (q i) o -> q g (i o)", i=ROWS),
            )
        nc.sync.dma_start(out=x_raw[0][:], in_=x_rows[:, :, 0:HALF])
        nc.sync.dma_start(out=x_raw[1][:], in_=x_rows[:, :, HALF:N])
        nc.sync.dma_start(out=v_raw[:], in_=v.rearrange("g (p j) o -> (g p) j o", j=PACK))
        nc.vector.memset(act_codes[:, 0:HALF], 0)
        nc.vector.memset(act_scales[:, 0:HALF], 0)
        nc.vector.tensor_copy(out=words_view(wq[0], 0, D), in_=rows_view(w_raw, 0, D))
        nc.vector.transpose(out=cols[:], in_=rows[:])
        quantize(wq)
        by_group = cols[:].rearrange("p (g i) -> p g i", i=ROWS)
        bias = by_group[:, :, 0]
        gain = by_group[:, :, 1]
        nc.vector.tensor_scalar(out=step[:], in0=gain, scalar1=0.0, scalar2=2.0, op0=ALU.is_ge, op1=ALU.mult)
        nc.vector.tensor_scalar(out=sign[:], in0=step[:], scalar1=-1.0, scalar2=None, op0=ALU.add)
        nc.scalar.activation(out=mag[:], in_=gain, func=ACT.Abs)
        for g in range(G):
            nc.scalar.activation(out=bmag[:, g : g + 1], in_=bias[:, g : g + 1], func=ACT.Copy, scale=mag[:, g : g + 1])

        def x_interleave(k, a, e, on_scalar):
            c0 = CHUNKS[k][0]
            copy = nc.scalar.copy if on_scalar else nc.vector.tensor_copy
            copy(out=words_view(xq[k][0], a, e), in_=rows_view(x_raw[c0 // HALF], c0 % HALF + a, c0 % HALF + e))

        def v_interleave():
            nc.vector.tensor_tensor(
                out=words_view(vq[0], 0, D),
                in0=rows_view(v_raw, 0, D),
                in1=sign[:].unsqueeze(1).unsqueeze(3).to_broadcast([P, D // 4, PACK, 4]),
                op=ALU.mult,
            )

        def product(bank, weights, slot):
            cols = slice((slot - 1) * HALF, (slot + 1) * HALF)
            for g in range(G):
                part = slice(ROWS * g, ROWS * (g + 1))
                nc.tensor.matmul_mx(
                    out=bank[g][:],
                    lhsT=weights[1][part, :].bitcast(FP8X4),
                    lhsT_scale=weights[2][part, :],
                    rhs=act_codes[part, cols].bitcast(FP8X4),
                    rhs_scale=act_scales[part, cols],
                    start=True,
                    stop=True,
                )

        def x_quant(k):
            quantize(xq[k])
            product(banks[Z_BANK[k]], wq, 1 + k)

        def z_out(k, g, on_scalar):
            c0, width = CHUNKS[k]
            src = banks[Z_BANK[k]][g][:, HALF:N]
            if on_scalar:
                nc.scalar.activation(out=h_bf[k][:, g, :], in_=src, func=ACT.Relu, bias=bmag[:, g : g + 1], scale=mag[:, g : g + 1])
            else:
                nc.vector.tensor_scalar(out=h_bf[k][:, g, :], in0=src, scalar1=bias[:, g : g + 1], scalar2=mag[:, g : g + 1], op0=ALU.add, op1=ALU.mult)

        def u_interleave(k, a, e, on_scalar):
            dst = words_view(uq[k][0], a, e)
            src = rows_view(h_bf[k], a, e)
            if on_scalar:
                nc.scalar.activation(out=dst, in_=src, func=ACT.Relu)
            else:
                nc.vector.tensor_scalar(out=dst, in0=src, scalar1=0.0, scalar2=None, op0=ALU.max)

        def u_quant(k):
            quantize(uq[k])
            product(banks[Y_BANK[k]], vq, 3 + k)

        def y_out(k, g, on_scalar):
            c0, width = CHUNKS[k]
            copy = nc.scalar.copy if on_scalar else nc.vector.tensor_copy
            copy(out=y_f32[:, g, c0 : c0 + width], in_=banks[Y_BANK[k]][g][:, HALF:N])

        def y_deal(k, g, on_scalar):
            c0, width = CHUNKS[k]
            copy = nc.scalar.copy if on_scalar else nc.vector.tensor_copy
            copy(out=y_round[k][:, g, :], in_=banks[Y_BANK[k]][g][:, HALF:N])
            nc.sync.dma_start(out=y_dealt[k][ROWS * g : ROWS * (g + 1), :, :], in_=y_round[k][:, g, :])

        def y_store(g0, g1):
            nc.sync.dma_start(out=out_0.rearrange("(g o) n -> o g n", g=G)[:, g0:g1, :], in_=y_f32[:, g0:g1, :])

        def y_interleave(k, a, e, on_scalar):
            copy = nc.scalar.copy if on_scalar else nc.vector.tensor_copy
            copy(out=words_view(y_bf[k], a, e), in_=rows_view(y_dealt[k], a, e))

        def y_quant(k):
            c0, width = CHUNKS[k]
            nc.vector.quantize_mx(
                out=y_codes[:, c0 : c0 + width].bitcast(FP8X4), scales=y_scales[:, c0 : c0 + width], in_=y_bf[k][:]
            )

        def words_store(c0, c1):
            words = out_1.rearrange("r p n s -> (r p) (n s)").bitcast(I32)
            nc.scalar.dma_start(out=words[:, c0:c1], in_=y_codes[:, c0:c1].bitcast(I32))

        def scales_store(q, queue):
            scale_rows = out_2.rearrange("r t n -> (r t) n").bitcast(I32)
            queue.dma_start(out=scale_rows[4 * q : 4 * q + 4, :], in_=y_scales[ROWS * q : ROWS * q + 4, :].bitcast(I32))

        x_interleave(0, 0, 176, False)
        x_interleave(0, 176, HALF, True)
        x_quant(0)
        product(banks[1], wq, 1)
        x_interleave(1, 0, 176, False)
        x_interleave(1, 176, HALF, True)
        x_quant(1)
        v_interleave()
        for g in range(G):
            z_out(0, g, g < 3)
        product(banks[0], wq, 2)
        product(banks[0], wq, 2)
        quantize(vq)
        u_interleave(0, 0, HALF, False)
        for g in range(G):
            z_out(1, g, g < 3)
        u_quant(0)
        u_interleave(1, 0, 176, False)
        u_interleave(1, 176, HALF, True)
        u_quant(1)
        for g in range(G):
            y_deal(0, g, g % 2 == 0)
        for g in range(2):
            y_out(0, g, g % 2 == 0)
        for g in range(G):
            y_deal(1, g, g % 2 == 0)
        for g in range(2):
            y_out(1, g, g % 2 == 0)
        y_store(0, 2)
        for k in range(2):
            for g in range(2, 4):
                y_out(k, g, g % 2 == 0)
        y_store(2, 4)
        y_interleave(0, 0, 176, False)
        y_interleave(0, 176, HALF, True)
        y_quant(0)
        y_interleave(1, 0, 176, False)
        y_interleave(1, 176, HALF, True)
        words_store(0, HALF)
        y_quant(1)
        words_store(HALF, N)
        for q in range(G):
            scales_store(q, nc.sync if q < 2 else nc.scalar)
